import numpy as np
import ml_dtypes


def mxq(x, axis, fmt="e4m3"):
    dtype, down = {"e4m3": (ml_dtypes.float8_e4m3fn, 7), "e5m2": (ml_dtypes.float8_e5m2, 14)}[fmt]
    v = np.moveaxis(np.asarray(x, np.float32).astype(ml_dtypes.bfloat16).astype(np.float64), axis, -1)
    blocks = v.reshape(v.shape[:-1] + (-1, 32))
    amax = np.abs(blocks).max(-1, keepdims=True)
    byte = np.maximum(np.where(amax > 0, np.frexp(amax)[1] - 1 + 127, 0) - down, 1)
    scale = np.exp2(byte - 127.0)
    codes = (blocks / scale).astype(np.float32).astype(dtype).astype(np.float64)
    return np.moveaxis((codes * scale).reshape(v.shape), -1, axis)


WIDE = False


def mx_kscale(k):
    if not WIDE:
        return np.ones(k)
    levels = np.array([10, -10, 5, -5, 0])
    if k % 512:
        return np.exp2(np.random.permutation(np.resize(levels, k // 32))).repeat(32)
    a = np.empty((k // 512, 16))
    for p in range(k // 512):
        a[p, :8] = np.random.permutation(np.resize(levels, 8))
        for g in range(8):
            far = levels[np.abs(levels - a[p, g]) >= 10]
            a[p, g + 8] = far[np.random.randint(len(far))]
    return np.exp2(a.ravel()).repeat(32)


BF16 = ml_dtypes.bfloat16


def bf(x):
    return np.asarray(x, np.float32).astype(BF16)


def f64(x):
    return np.asarray(x).astype(np.float64)


M, G, D, C = 1024, 4, 512, 2048


def setup_inputs():
    s, t, u = mx_kscale(C), mx_kscale(C), mx_kscale(C)
    t_plain = t.reshape(D, G).T.reshape(C)
    u_shuf = u.reshape(G, D).T.reshape(C)
    w1 = 0.5 * np.random.standard_normal((G, D, D)) / np.sqrt(D)
    w2 = 0.5 * np.random.standard_normal((G, D, D)) / np.sqrt(D)
    w3 = np.random.standard_normal((G, D, D)) / np.sqrt(D)
    return {"x": bf(np.random.standard_normal((M, C)) * s),
            "w1": bf(w1 / s.reshape(G, D, 1) * t_plain.reshape(G, 1, D)),
            "a1": bf((1 + 0.1 * np.random.standard_normal(C)) * t_plain / s),
            "w2": bf(w2 / t.reshape(G, D, 1) * u_shuf.reshape(G, 1, D)),
            "a2": bf((1 + 0.1 * np.random.standard_normal(C)) * u_shuf / t),
            "w3": bf(w3 / u.reshape(G, D, 1))}


def reference(x, w1, a1, w2, a2, w3):
    x = f64(x)
    h1 = mxq(x.reshape(M, G, D).swapaxes(0, 1), 2, "e4m3") @ mxq(f64(w1), 1, "e4m3")
    y1 = x * f64(a1) + np.maximum(h1.swapaxes(0, 1).reshape(M, C), 0)
    z = y1.reshape(M, G, D).swapaxes(1, 2).reshape(M, C)
    h2 = mxq(z.reshape(M, G, D).swapaxes(0, 1), 2, "e4m3") @ mxq(f64(w2), 1, "e4m3")
    v = z * f64(a2) + np.maximum(h2.swapaxes(0, 1).reshape(M, C), 0)
    y2 = v.reshape(M, D, G).swapaxes(1, 2).reshape(M, C)
    h3 = mxq(y2.reshape(M, G, D).swapaxes(0, 1), 2, "e4m3") @ mxq(f64(w3), 1, "e4m3")
    return h3.swapaxes(0, 1).reshape(M, C)

@@ -1,0 +1,336 @@
+from contextlib import ExitStack
+
+import concourse.mybir as mybir
+from concourse.masks import make_identity
+
+M, C, G, D = 1024, 2048, 4, 512
+FLOPS = 3 * 2 * M * C * D
+
+F32 = mybir.dt.float32
+BF16 = mybir.dt.bfloat16
+U32 = mybir.dt.uint32
+U8 = mybir.dt.uint8
+FP8X4 = mybir.dt.float8_e4m3fn_x4
+ALU = mybir.AluOpType
+COPY = mybir.ActivationFunctionType.Copy
+
+P = 128
+CHUNKS = [(0, 4), (4, 4)]
+SKIP_G = (0, 1, 2, 3)
+ZA = 2
+CAST = "SSSSSSSS"
+PRO = """I10V W00 q10 L20 W01 x00 I11V L21 W02 x01 q11 g00 W03 I12V I13S L22 x02 q12 x03 L23 N00 I20V q13 Z00
+X04 X05 X06 X07 X14 X15 X16 X17 L30 L31 """
+PRE = ["","","","","","","","",""]
+MID = ["I21V q20 W10","I22V q21 x10 W11 L32","I23V q22 x11 W12 W13","q23 x12 x13 I30V L33","I31V q30","I32V q31 T00 T01 Y00","I33V q32 y00 T02 Y01 T03","q33 y01 O00 Y02","y02 O01 Y03"]
+POST = ["","","","","","","","",""]
+END = """T10SV T11SV O02 y03 Y10SV T12SV O03SVSV y10 Y11SV T13SV O10SVSV y11 Y12SV O11SVSV y12 Y13SV O12SVSV y13 O13SVSV"""
+
+
+def tile_group_shuffled_channel_mixer_t1_kernel(tc, x, w1, a1, w2, a2, w3, out):
+    nc = tc.nc
+    with ExitStack() as ctx:
+        keep = ctx.enter_context(tc.tile_pool(name="keep", bufs=1))
+        sb = ctx.enter_context(tc.tile_pool(name="sb", bufs=2))
+        psum = ctx.enter_context(tc.psum_pool(name="psum", bufs=8))
+        ctx.enter_context(tc.manual_schedule())
+
+        def bank(shape, dtype):
+            return psum.tile(shape, dtype, name="bank", tag="bank", bufs=8)
+
+        def copy(engine, dst, src):
+            if engine == "S":
+                nc.scalar.copy(dst, src)
+            elif engine == "G":
+                nc.gpsimd.tensor_scalar(out=dst, in0=src, scalar1=1.0, scalar2=0.0, op0=ALU.mult, op1=ALU.add)
+            else:
+                nc.vector.tensor_copy(dst, src)
+
+        xt = {}
+        wraw = {}
+
+        def load_x(half, b):
+            t = sb.tile([P, 1024], BF16, name="xt", tag="xt", bufs=16, align_bytes=64)
+            nc.sync.dma_start(out=t[:], in_=x[b * P : b * P + P, half * 1024 : half * 1024 + 1024])
+            xt[half, b] = t
+
+        weights = {1: w1, 2: w2, 3: w3}
+
+        def load_w(k, i):
+            t = sb.tile([P, 4, D], BF16, name="wraw", tag="wraw", bufs=6, align_bytes=64)
+            nc.sync.dma_start(out=t[:], in_=weights[k][i].rearrange("(p j) c -> p j c", j=4))
+            wraw[k, i] = t
+
+        wb, wc, ws = {}, {}, {}
+
+        def interleave_w(engine, k, i):
+            t = sb.tile([P, 4 * D], BF16, name="wb", tag="wb", bufs=2, align_bytes=64)
+            if k == 2:
+                dst = t[:].rearrange("p (t m j) -> p t m j", t=4, j=4)
+                src = wraw[k, i][:].rearrange("p j (m t) -> p t m j", t=4)
+            else:
+                dst = t[:].rearrange("p (c e j) -> p c j e", e=4, j=4)
+                src = wraw[k, i][:].rearrange("p j (c e) -> p c j e", e=4)
+            pieces = 4 if engine == "G" else 1
+            n = dst.shape[1] // pieces
+            for q in range(pieces):
+                copy(engine, dst[:, q * n : q * n + n], src[:, q * n : q * n + n])
+            wb[k, i] = t
+
+        def quantize_w(k, i):
+            c = keep.tile([P, D], U32, name="wc%d%d" % (k, i), align_bytes=64)
+            s = keep.tile([P, D], U8, name="ws%d%d" % (k, i), align_bytes=64)
+            nc.vector.quantize_mx(out=c[:].bitcast(FP8X4), scales=s[:], in_=wb[k, i][:])
+            wc[k, i], ws[k, i] = c, s
+
+        def turn_words(words, dst, engine):
+            ps = bank([P, 2, 2, P], F32)
+            for b in range(2):
+                for u in range(2):
+                    nc.tensor.transpose(ps[:, b, u, :], words[b][u], ident_f[:])
+            copy(engine, dst.rearrange("p (b r u) -> p b r u", b=2, u=2), ps[:].rearrange("p b u r -> p b r u"))
+
+        xb, xc, xs = {}, {}, {}
+
+        def turn_x(h, i, engines="SS"):
+            b0, nb = CHUNKS[h]
+            t = sb.tile([P, 4 * P * nb], BF16, name="kb", tag="kb", bufs=2, align_bytes=64)
+            w0 = (i % 2) * 256
+            for pr in range(nb // 2):
+                words = []
+                for b in range(2):
+                    v = xt[i // 2, b0 + 2 * pr + b][:].bitcast(F32)
+                    words.append([v[:, w0 + u : w0 + 256 : 2] for u in range(2)])
+                turn_words(words, t[:].bitcast(F32)[:, pr * 512 : pr * 512 + 512], engines[pr])
+            xb[h, i] = t
+
+        def quantize_x(h, i):
+            nt = P * CHUNKS[h][1]
+            c = sb.tile([P, nt], U32, name="xc", tag="xc", bufs=8, align_bytes=64)
+            s = sb.tile([P, nt], U8, name="xs", tag="xs", bufs=8, align_bytes=64)
+            nc.vector.quantize_mx(out=c[:].bitcast(FP8X4), scales=s[:], in_=xb[h, i][:])
+            xc[h, i], xs[h, i] = c, s
+
+        h1 = {}
+        zf, zb, zc, zs, za, yb16 = {}, {}, {}, {}, {}, {}
+
+        def skip_x(h, g):
+            b0, nb = CHUNKS[h]
+            nt = P * nb
+            t = sb.tile([P, G, nt], F32, name="zf", tag="zf", bufs=4, align_bytes=64)
+            for half in range(2):
+                ps = bank([P, 2, nt], BF16)
+                for e in range(2):
+                    c0 = e * D + g * P
+                    for b in range(nb):
+                        nc.tensor.transpose(ps[:, e, b * P : b * P + P], xt[half, b0 + b][:, c0 : c0 + P], ident_b[:])
+                for e in range(2):
+                    i = 2 * half + e
+                    r = i * G + g
+                    nc.scalar.activation(out=t[:, i, :], in_=ps[:, e, :], func=COPY, scale=gain1[:, r : r + 1])
+            zf[h, g] = t
+
+        def stage1(h, g):
+            for i in range(G):
+                ps = bank([P, P * CHUNKS[h][1]], F32)
+                nc.tensor.matmul_mx(
+                    out=ps[:],
+                    lhsT=wc[1, i][:, g * P : g * P + P].bitcast(FP8X4),
+                    lhsT_scale=ws[1, i][:, g * P : g * P + P],
+                    rhs=xc[h, i][:].bitcast(FP8X4),
+                    rhs_scale=xs[h, i][:],
+                    start=True,
+                    stop=True,
+                )
+                h1[h, g, i] = ps
+
+        def finish1(h, g):
+            for i in range(G):
+                z = zf[h, g][:, i, :]
+                ps = h1[h, g, i]
+                nc.vector.scalar_tensor_tensor(out=z, in0=ps[:], scalar=0.0, in1=z, op0=ALU.max, op1=ALU.add)
+
+        def cast_z(engine, h, g):
+            t = sb.tile([P, P * CHUNKS[h][1], G], BF16, name="zb", tag="zb", bufs=2, align_bytes=64)
+            copy(engine, t[:], zf[h, g][:].rearrange("p i n -> p n i"))
+            zb[h, g] = t
+
+        def quantize_z(h, g):
+            nt = P * CHUNKS[h][1]
+            c = sb.tile([P, nt], U32, name="zc", tag="zc", bufs=2, align_bytes=64)
+            s = sb.tile([P, nt], U8, name="zs", tag="zs", bufs=2, align_bytes=64)
+            nc.vector.quantize_mx(out=c[:].bitcast(FP8X4), scales=s[:], in_=zb[h, g][:].rearrange("p n i -> p (n i)"))
+            zc[h, g], zs[h, g] = c, s
+
+        def skip_z(h, g):
+            t = sb.tile([P, G, P * CHUNKS[h][1]], F32, name="za", tag="za", bufs=ZA, align_bytes=64)
+            for i in range(G):
+                if i in SKIP_G:
+                    nc.gpsimd.tensor_scalar(out=t[:, i, :], in0=zf[h, g][:, i, :], scalar1=gain2[:, i, g : g + 1], scalar2=0.0, op0=ALU.mult, op1=ALU.add)
+                else:
+                    nc.vector.tensor_scalar(out=t[:, i, :], in0=zf[h, g][:, i, :], scalar1=gain2[:, i, g : g + 1], scalar2=None, op0=ALU.mult)
+            za[h, g] = t
+
+        late = {}
+
+        def stage2(h, g):
+            nt = P * CHUNKS[h][1]
+            t = sb.tile([P, G, nt], BF16, name="y2", tag="y2", bufs=8, align_bytes=64)
+            for i in range(G):
+                ps = bank([P, nt], F32)
+                nc.tensor.matmul_mx(
+                    out=ps[:],
+                    lhsT=wc[2, g][:, i * P : i * P + P].bitcast(FP8X4),
+                    lhsT_scale=ws[2, g][:, i * P : i * P + P],
+                    rhs=zc[h, g][:].bitcast(FP8X4),
+                    rhs_scale=zs[h, g][:],
+                    start=True,
+                    stop=True,
+                )
+                late[h, g, i] = (t[:, i, :], ps[:], za[h, g][:, i, :])
+            yb16[h, g] = t
+
+        def finish2(h, g, parts):
+            for i in parts:
+                o, a, b = late[h, g, i]
+                nc.vector.scalar_tensor_tensor(out=o, in0=a, scalar=0.0, in1=b, op0=ALU.max, op1=ALU.add)
+
+        yt, yk, yc, ys = {}, {}, {}, {}
+
+        def turn_back(h, i, engines="SS"):
+            for pr in range(CHUNKS[h][1] // 2):
+                ps = bank([P, 2, D], BF16)
+                for b in range(2):
+                    n0 = (2 * pr + b) * P
+                    for g in range(G):
+                        nc.tensor.transpose(ps[:, b, g * P : g * P + P], yb16[h, g][:, i, n0 : n0 + P], ident_b[:])
+                t = sb.tile([P, 2, D], BF16, name="yt", tag="yt", bufs=4, align_bytes=64)
+                copy(
+                    engines[pr],
+                    t[:].rearrange("p b d -> p (b d)").bitcast(F32).rearrange("p (b u r) -> p b u r", b=2, u=2),
+                    ps[:].rearrange("p b d -> p (b d)").bitcast(F32).rearrange("p (b r u) -> p b u r", b=2, u=2),
+                )
+                yt[h, i, pr] = t
+
+        def turn_y(h, i, engines="SS"):
+            nb = CHUNKS[h][1]
+            t = sb.tile([P, 4 * P * nb], BF16, name="kb", tag="kb", bufs=2, align_bytes=64)
+            for pr in range(nb // 2):
+                v = yt[h, i, pr][:].rearrange("p b d -> p (b d)").bitcast(F32)
+                words = [[v[:, 256 * b + 128 * u : 256 * b + 128 * u + 128] for u in range(2)] for b in range(2)]
+                turn_words(words, t[:].bitcast(F32)[:, pr * 512 : pr * 512 + 512], engines[pr])
+            yk[h, i] = t
+
+        def quantize_y(h, i):
+            nt = P * CHUNKS[h][1]
+            c = sb.tile([P, nt], U32, name="yc", tag="yc", bufs=3, align_bytes=64)
+            s = sb.tile([P, nt], U8, name="ys", tag="ys", bufs=3, align_bytes=64)
+            nc.vector.quantize_mx(out=c[:].bitcast(FP8X4), scales=s[:], in_=yk[h, i][:])
+            yc[h, i], ys[h, i] = c, s
+
+        def stage3(h, i, engines="SSSS"):
+            b0, nb = CHUNKS[h]
+            for b in range(nb):
+                ps = bank([P, D], F32)
+                nc.tensor.matmul_mx(
+                    out=ps[:],
+                    lhsT=yc[h, i][:, b * P : b * P + P].bitcast(FP8X4),
+                    lhsT_scale=ys[h, i][:, b * P : b * P + P],
+                    rhs=wc[3, i][:].bitcast(FP8X4),
+                    rhs_scale=ws[3, i][:],
+                    start=True,
+                    stop=True,
+                )
+                t = sb.tile([P, D], F32, name="ot", tag="wraw", bufs=6, align_bytes=64)
+                copy(engines[b], t[:], ps[:])
+                r0 = (b0 + b) * P
+                nc.sync.dma_start(out=out[r0 : r0 + P, i * D : i * D + D], in_=t[:])
+
+        raw1 = keep.tile([P, P], BF16, name="raw1", align_bytes=64)
+        raw2 = keep.tile([P, D], BF16, name="raw2", align_bytes=64)
+        nc.vector.memset(raw1[:], 0.0)
+        nc.vector.memset(raw2[:], 0.0)
+        ident_b = keep.tile([P, P], BF16, name="ident_b", align_bytes=64)
+        ident_f = keep.tile([P, P], F32, name="ident_f", align_bytes=64)
+        make_identity(nc, ident_f[:])
+        make_identity(nc, ident_b[:])
+        nc.scalar.dma_start(out=raw1[0:16, :], in_=a1.rearrange("(r p) -> r p", p=P))
+        nc.scalar.dma_start(out=raw2[0:4, :], in_=a2.rearrange("(g c) -> g c", c=D))
+        for u in "L10 X00 X01 X02 X03 L11 X10 X11 X12 X13 L12 L13".split():
+            if u[0] == "L":
+                load_w(int(u[1]), int(u[2]))
+            else:
+                load_x(int(u[1]), int(u[2]))
+        gain1 = keep.tile([P, 16], F32, name="gain1", align_bytes=64)
+        gain2 = keep.tile([P, G, G], F32, name="gain2", align_bytes=64)
+
+        def turn_gains():
+            gps = bank([P, 5, P], BF16)
+            nc.tensor.transpose(gps[:, 0, :], raw1[:], ident_b[:])
+            for i in range(G):
+                nc.tensor.transpose(gps[:, 1 + i, :], raw2[:, i : D : 4], ident_b[:])
+            nc.vector.tensor_copy(gain1[:], gps[:, 0, 0:16])
+            nc.vector.tensor_copy(gain2[:], gps[:, 1:5, 0:4])
+
+        def unit(u):
+            kind, h, i = u[0], int(u[1]), int(u[2])
+            e = u[3:]
+            if kind == "L":
+                load_w(h, i)
+            elif kind == "X":
+                load_x(h, i)
+            elif kind == "I":
+                interleave_w(e, h, i)
+            elif kind == "q":
+                quantize_w(h, i)
+            elif kind == "W":
+                turn_x(h, i, e or "SS")
+            elif kind == "x":
+                quantize_x(h, i)
+            elif kind == "T":
+                turn_back(h, i, e or "SS")
+            elif kind == "Y":
+                turn_y(h, i, e or "SS")
+            elif kind == "y":
+                quantize_y(h, i)
+            elif kind == "O":
+                stage3(h, i, e or "SSSS")
+            elif kind == "g":
+                turn_gains()
+            elif kind == "N":
+                skip_x(h, i)
+            elif kind == "Z":
+                stage1(h, i)
+
+        for u in PRO.split():
+            unit(u)
+        steps = [(h, g) for h in range(len(CHUNKS)) for g in range(G)]
+        for s in range(len(steps) + 1):
+            this = steps[s] if s < len(steps) else None
+            prev = steps[s - 1] if s > 0 else None
+            nxt = steps[s + 1] if s + 1 < len(steps) else None
+            if nxt:
+                skip_x(*nxt)
+            if this:
+                finish1(*this)
+            for u in PRE[s].split():
+                unit(u)
+            if this and CAST[s] == "V":
+                cast_z("V", *this)
+            if prev:
+                quantize_z(*prev)
+                stage2(*prev)
+            if this and CAST[s] != "V":
+                cast_z(CAST[s], *this)
+            if this:
+                skip_z(*this)
+            for u in MID[s].split():
+                unit(u)
+            if nxt:
+                stage1(*nxt)
+            if prev:
+                finish2(*prev, range(G))
+            for u in POST[s].split():
+                unit(u)
+        for u in END.split():
+            unit(u)

@@ -19,12 +19,11 @@ CHUNKS = [(0, 4), (4, 4)]
 SKIP_G = (0, 1, 2, 3)
 ZA = 2
 CAST = "SSSSSSSS"
-PRO = """I10V W00 q10 L20 W01 x00 I11V L21 W02 x01 q11 g00 W03 I12V I13S L22 x02 q12 x03 L23 N00 I20V q13 Z00
-X04 X05 X06 X07 X14 X15 X16 X17 L30 L31 """
-PRE = ["","","","","","","","",""]
-MID = ["I21V q20 W10","I22V q21 x10 W11 L32","I23V q22 x11 W12 W13","q23 x12 x13 I30V L33","I31V q30","I32V q31 T00 T01 Y00","I33V q32 y00 T02 Y01 T03","q33 y01 O00 Y02","y02 O01 Y03"]
-POST = ["","","","","","","","",""]
-END = """T10SV T11SV O02 y03 Y10SV T12SV O03SVSV y10 Y11SV T13SV O10SVSV y11 Y12SV O11SVSV y12 Y13SV O12SVSV y13 O13SVSV"""
+PRO = """I10V W01VV I11V x01 q11 W00SS W02SS W03SS L22 L20 q10 I13S I12V x00 g00 x03 q12 q13 N00 x02 Z00 X04"""
+PRE = ["L23 X06 I20V X15 I22V","W11","X14","x10 x12 L32","","Y00VV T02","I32V","T03",""]
+MID = ["X05 X16 X17 L31 L33","I23S L21 I21V","q23 x11 W13","x13","I31V","q31","T01 q30","y00 Y01","I33V y01 O01SSSS"]
+POST = ["q20 X07 q22","L30 q21 W10","W12","","I30S T00SS","Y02","","O00SSSS y02","q32 T10VS Y03SV O02SVSV T11SS y03 q33 Y10VV Y11SV y10 y11 O03SSSV T13SV"]
+END = """O10SVSV T12SS Y13VV O11SVSS y13 Y12VS O13VSSS y12 O12VVSS"""
 
 
 def tile_group_shuffled_channel_mixer_t1_kernel(tc, x, w1, a1, w2, a2, w3, out):
@@ -94,7 +93,7 @@ def tile_group_shuffled_channel_mixer_t1_kernel(tc, x, w1, a1, w2, a2, w3, out):
 
         def turn_x(h, i, engines="SS"):
             b0, nb = CHUNKS[h]
-            t = sb.tile([P, 4 * P * nb], BF16, name="kb", tag="kb", bufs=2, align_bytes=64)
+            t = sb.tile([P, 4 * P * nb], BF16, name="kb", tag="kb", bufs=3, align_bytes=64)
             w0 = (i % 2) * 256
             for pr in range(nb // 2):
                 words = []
@@ -214,7 +213,7 @@ def tile_group_shuffled_channel_mixer_t1_kernel(tc, x, w1, a1, w2, a2, w3, out):
 
         def turn_y(h, i, engines="SS"):
             nb = CHUNKS[h][1]
-            t = sb.tile([P, 4 * P * nb], BF16, name="kb", tag="kb", bufs=2, align_bytes=64)
+            t = sb.tile([P, 4 * P * nb], BF16, name="kb", tag="kb", bufs=3, align_bytes=64)
             for pr in range(nb // 2):
                 v = yt[h, i, pr][:].rearrange("p b d -> p (b d)").bitcast(F32)
                 words = [[v[:, 256 * b + 128 * u : 256 * b + 128 * u + 128] for u in range(2)] for b in range(2)]

from contextlib import ExitStack

import concourse.mybir as mybir
from concourse.masks import make_identity

M, C, G, D = 1024, 2048, 4, 512
FLOPS = 3 * 2 * M * C * D

F32 = mybir.dt.float32
BF16 = mybir.dt.bfloat16
U32 = mybir.dt.uint32
U8 = mybir.dt.uint8
FP8X4 = mybir.dt.float8_e4m3fn_x4
ALU = mybir.AluOpType
COPY = mybir.ActivationFunctionType.Copy

P = 128
CHUNKS = [(0, 4), (4, 4)]
SKIP_G = (0, 1, 2, 3)
ZA = 2
CAST = "SSSSSSSS"
PRO = """I10V W01VV I11V x01 q11 W00SS W02SS W03SS L22 L20 q10 I13S I12V x00 g00 x03 q12 q13 N00 x02 Z00 X04"""
PRE = ["L23 X06 I20V X15 I22V","W11","X14","x10 x12 L32","","Y00VV T02","I32V","T03",""]
MID = ["X05 X16 X17 L31 L33","I23S L21 I21V","q23 x11 W13","x13","I31V","q31","T01 q30","y00 Y01","I33V y01 O01SSSS"]
POST = ["q20 X07 q22","L30 q21 W10","W12","","I30S T00SS","Y02","","O00SSSS y02","q32 T10VS Y03SV O02SVSV T11SS y03 q33 Y10VV Y11SV y10 y11 O03SSSV T13SV"]
END = """O10SVSV T12SS Y13VV O11SVSS y13 Y12VS O13VSSS y12 O12VVSS"""


def tile_group_shuffled_channel_mixer_t1_kernel(tc, x, w1, a1, w2, a2, w3, out):
    nc = tc.nc
    with ExitStack() as ctx:
        keep = ctx.enter_context(tc.tile_pool(name="keep", bufs=1))
        sb = ctx.enter_context(tc.tile_pool(name="sb", bufs=2))
        psum = ctx.enter_context(tc.psum_pool(name="psum", bufs=8))
        ctx.enter_context(tc.manual_schedule())

        def bank(shape, dtype):
            return psum.tile(shape, dtype, name="bank", tag="bank", bufs=8)

        def copy(engine, dst, src):
            if engine == "S":
                nc.scalar.copy(dst, src)
            elif engine == "G":
                nc.gpsimd.tensor_scalar(out=dst, in0=src, scalar1=1.0, scalar2=0.0, op0=ALU.mult, op1=ALU.add)
            else:
                nc.vector.tensor_copy(dst, src)

        xt = {}
        wraw = {}

        def load_x(half, b):
            t = sb.tile([P, 1024], BF16, name="xt", tag="xt", bufs=16, align_bytes=64)
            nc.sync.dma_start(out=t[:], in_=x[b * P : b * P + P, half * 1024 : half * 1024 + 1024])
            xt[half, b] = t

        weights = {1: w1, 2: w2, 3: w3}

        def load_w(k, i):
            t = sb.tile([P, 4, D], BF16, name="wraw", tag="wraw", bufs=6, align_bytes=64)
            nc.sync.dma_start(out=t[:], in_=weights[k][i].rearrange("(p j) c -> p j c", j=4))
            wraw[k, i] = t

        wb, wc, ws = {}, {}, {}

        def interleave_w(engine, k, i):
            t = sb.tile([P, 4 * D], BF16, name="wb", tag="wb", bufs=2, align_bytes=64)
            if k == 2:
                dst = t[:].rearrange("p (t m j) -> p t m j", t=4, j=4)
                src = wraw[k, i][:].rearrange("p j (m t) -> p t m j", t=4)
            else:
                dst = t[:].rearrange("p (c e j) -> p c j e", e=4, j=4)
                src = wraw[k, i][:].rearrange("p j (c e) -> p c j e", e=4)
            pieces = 4 if engine == "G" else 1
            n = dst.shape[1] // pieces
            for q in range(pieces):
                copy(engine, dst[:, q * n : q * n + n], src[:, q * n : q * n + n])
            wb[k, i] = t

        def quantize_w(k, i):
            c = keep.tile([P, D], U32, name="wc%d%d" % (k, i), align_bytes=64)
            s = keep.tile([P, D], U8, name="ws%d%d" % (k, i), align_bytes=64)
            nc.vector.quantize_mx(out=c[:].bitcast(FP8X4), scales=s[:], in_=wb[k, i][:])
            wc[k, i], ws[k, i] = c, s

        def turn_words(words, dst, engine):
            ps = bank([P, 2, 2, P], F32)
            for b in range(2):
                for u in range(2):
                    nc.tensor.transpose(ps[:, b, u, :], words[b][u], ident_f[:])
            copy(engine, dst.rearrange("p (b r u) -> p b r u", b=2, u=2), ps[:].rearrange("p b u r -> p b r u"))

        xb, xc, xs = {}, {}, {}

        def turn_x(h, i, engines="SS"):
            b0, nb = CHUNKS[h]
            t = sb.tile([P, 4 * P * nb], BF16, name="kb", tag="kb", bufs=3, align_bytes=64)
            w0 = (i % 2) * 256
            for pr in range(nb // 2):
                words = []
                for b in range(2):
                    v = xt[i // 2, b0 + 2 * pr + b][:].bitcast(F32)
                    words.append([v[:, w0 + u : w0 + 256 : 2] for u in range(2)])
                turn_words(words, t[:].bitcast(F32)[:, pr * 512 : pr * 512 + 512], engines[pr])
            xb[h, i] = t

        def quantize_x(h, i):
            nt = P * CHUNKS[h][1]
            c = sb.tile([P, nt], U32, name="xc", tag="xc", bufs=8, align_bytes=64)
            s = sb.tile([P, nt], U8, name="xs", tag="xs", bufs=8, align_bytes=64)
            nc.vector.quantize_mx(out=c[:].bitcast(FP8X4), scales=s[:], in_=xb[h, i][:])
            xc[h, i], xs[h, i] = c, s

        h1 = {}
        zf, zb, zc, zs, za, yb16 = {}, {}, {}, {}, {}, {}

        def skip_x(h, g):
            b0, nb = CHUNKS[h]
            nt = P * nb
            t = sb.tile([P, G, nt], F32, name="zf", tag="zf", bufs=4, align_bytes=64)
            for half in range(2):
                ps = bank([P, 2, nt], BF16)
                for e in range(2):
                    c0 = e * D + g * P
                    for b in range(nb):
                        nc.tensor.transpose(ps[:, e, b * P : b * P + P], xt[half, b0 + b][:, c0 : c0 + P], ident_b[:])
                for e in range(2):
                    i = 2 * half + e
                    r = i * G + g
                    nc.scalar.activation(out=t[:, i, :], in_=ps[:, e, :], func=COPY, scale=gain1[:, r : r + 1])
            zf[h, g] = t

        def stage1(h, g):
            for i in range(G):
                ps = bank([P, P * CHUNKS[h][1]], F32)
                nc.tensor.matmul_mx(
                    out=ps[:],
                    lhsT=wc[1, i][:, g * P : g * P + P].bitcast(FP8X4),
                    lhsT_scale=ws[1, i][:, g * P : g * P + P],
                    rhs=xc[h, i][:].bitcast(FP8X4),
                    rhs_scale=xs[h, i][:],
                    start=True,
                    stop=True,
                )
                h1[h, g, i] = ps

        def finish1(h, g):
            for i in range(G):
                z = zf[h, g][:, i, :]
                ps = h1[h, g, i]
                nc.vector.scalar_tensor_tensor(out=z, in0=ps[:], scalar=0.0, in1=z, op0=ALU.max, op1=ALU.add)

        def cast_z(engine, h, g):
            t = sb.tile([P, P * CHUNKS[h][1], G], BF16, name="zb", tag="zb", bufs=2, align_bytes=64)
            copy(engine, t[:], zf[h, g][:].rearrange("p i n -> p n i"))
            zb[h, g] = t

        def quantize_z(h, g):
            nt = P * CHUNKS[h][1]
            c = sb.tile([P, nt], U32, name="zc", tag="zc", bufs=2, align_bytes=64)
            s = sb.tile([P, nt], U8, name="zs", tag="zs", bufs=2, align_bytes=64)
            nc.vector.quantize_mx(out=c[:].bitcast(FP8X4), scales=s[:], in_=zb[h, g][:].rearrange("p n i -> p (n i)"))
            zc[h, g], zs[h, g] = c, s

        def skip_z(h, g):
            t = sb.tile([P, G, P * CHUNKS[h][1]], F32, name="za", tag="za", bufs=ZA, align_bytes=64)
            for i in range(G):
                if i in SKIP_G:
                    nc.gpsimd.tensor_scalar(out=t[:, i, :], in0=zf[h, g][:, i, :], scalar1=gain2[:, i, g : g + 1], scalar2=0.0, op0=ALU.mult, op1=ALU.add)
                else:
                    nc.vector.tensor_scalar(out=t[:, i, :], in0=zf[h, g][:, i, :], scalar1=gain2[:, i, g : g + 1], scalar2=None, op0=ALU.mult)
            za[h, g] = t

        late = {}

        def stage2(h, g):
            nt = P * CHUNKS[h][1]
            t = sb.tile([P, G, nt], BF16, name="y2", tag="y2", bufs=8, align_bytes=64)
            for i in range(G):
                ps = bank([P, nt], F32)
                nc.tensor.matmul_mx(
                    out=ps[:],
                    lhsT=wc[2, g][:, i * P : i * P + P].bitcast(FP8X4),
                    lhsT_scale=ws[2, g][:, i * P : i * P + P],
                    rhs=zc[h, g][:].bitcast(FP8X4),
                    rhs_scale=zs[h, g][:],
                    start=True,
                    stop=True,
                )
                late[h, g, i] = (t[:, i, :], ps[:], za[h, g][:, i, :])
            yb16[h, g] = t

        def finish2(h, g, parts):
            for i in parts:
                o, a, b = late[h, g, i]
                nc.vector.scalar_tensor_tensor(out=o, in0=a, scalar=0.0, in1=b, op0=ALU.max, op1=ALU.add)

        yt, yk, yc, ys = {}, {}, {}, {}

        def turn_back(h, i, engines="SS"):
            for pr in range(CHUNKS[h][1] // 2):
                ps = bank([P, 2, D], BF16)
                for b in range(2):
                    n0 = (2 * pr + b) * P
                    for g in range(G):
                        nc.tensor.transpose(ps[:, b, g * P : g * P + P], yb16[h, g][:, i, n0 : n0 + P], ident_b[:])
                t = sb.tile([P, 2, D], BF16, name="yt", tag="yt", bufs=4, align_bytes=64)
                copy(
                    engines[pr],
                    t[:].rearrange("p b d -> p (b d)").bitcast(F32).rearrange("p (b u r) -> p b u r", b=2, u=2),
                    ps[:].rearrange("p b d -> p (b d)").bitcast(F32).rearrange("p (b r u) -> p b u r", b=2, u=2),
                )
                yt[h, i, pr] = t

        def turn_y(h, i, engines="SS"):
            nb = CHUNKS[h][1]
            t = sb.tile([P, 4 * P * nb], BF16, name="kb", tag="kb", bufs=3, align_bytes=64)
            for pr in range(nb // 2):
                v = yt[h, i, pr][:].rearrange("p b d -> p (b d)").bitcast(F32)
                words = [[v[:, 256 * b + 128 * u : 256 * b + 128 * u + 128] for u in range(2)] for b in range(2)]
                turn_words(words, t[:].bitcast(F32)[:, pr * 512 : pr * 512 + 512], engines[pr])
            yk[h, i] = t

        def quantize_y(h, i):
            nt = P * CHUNKS[h][1]
            c = sb.tile([P, nt], U32, name="yc", tag="yc", bufs=3, align_bytes=64)
            s = sb.tile([P, nt], U8, name="ys", tag="ys", bufs=3, align_bytes=64)
            nc.vector.quantize_mx(out=c[:].bitcast(FP8X4), scales=s[:], in_=yk[h, i][:])
            yc[h, i], ys[h, i] = c, s

        def stage3(h, i, engines="SSSS"):
            b0, nb = CHUNKS[h]
            for b in range(nb):
                ps = bank([P, D], F32)
                nc.tensor.matmul_mx(
                    out=ps[:],
                    lhsT=yc[h, i][:, b * P : b * P + P].bitcast(FP8X4),
                    lhsT_scale=ys[h, i][:, b * P : b * P + P],
                    rhs=wc[3, i][:].bitcast(FP8X4),
                    rhs_scale=ws[3, i][:],
                    start=True,
                    stop=True,
                )
                t = sb.tile([P, D], F32, name="ot", tag="wraw", bufs=6, align_bytes=64)
                copy(engines[b], t[:], ps[:])
                r0 = (b0 + b) * P
                nc.sync.dma_start(out=out[r0 : r0 + P, i * D : i * D + D], in_=t[:])

        raw1 = keep.tile([P, P], BF16, name="raw1", align_bytes=64)
        raw2 = keep.tile([P, D], BF16, name="raw2", align_bytes=64)
        nc.vector.memset(raw1[:], 0.0)
        nc.vector.memset(raw2[:], 0.0)
        ident_b = keep.tile([P, P], BF16, name="ident_b", align_bytes=64)
        ident_f = keep.tile([P, P], F32, name="ident_f", align_bytes=64)
        make_identity(nc, ident_f[:])
        make_identity(nc, ident_b[:])
        nc.scalar.dma_start(out=raw1[0:16, :], in_=a1.rearrange("(r p) -> r p", p=P))
        nc.scalar.dma_start(out=raw2[0:4, :], in_=a2.rearrange("(g c) -> g c", c=D))
        for u in "L10 X00 X01 X02 X03 L11 X10 X11 X12 X13 L12 L13".split():
            if u[0] == "L":
                load_w(int(u[1]), int(u[2]))
            else:
                load_x(int(u[1]), int(u[2]))
        gain1 = keep.tile([P, 16], F32, name="gain1", align_bytes=64)
        gain2 = keep.tile([P, G, G], F32, name="gain2", align_bytes=64)

        def turn_gains():
            gps = bank([P, 5, P], BF16)
            nc.tensor.transpose(gps[:, 0, :], raw1[:], ident_b[:])
            for i in range(G):
                nc.tensor.transpose(gps[:, 1 + i, :], raw2[:, i : D : 4], ident_b[:])
            nc.vector.tensor_copy(gain1[:], gps[:, 0, 0:16])
            nc.vector.tensor_copy(gain2[:], gps[:, 1:5, 0:4])

        def unit(u):
            kind, h, i = u[0], int(u[1]), int(u[2])
            e = u[3:]
            if kind == "L":
                load_w(h, i)
            elif kind == "X":
                load_x(h, i)
            elif kind == "I":
                interleave_w(e, h, i)
            elif kind == "q":
                quantize_w(h, i)
            elif kind == "W":
                turn_x(h, i, e or "SS")
            elif kind == "x":
                quantize_x(h, i)
            elif kind == "T":
                turn_back(h, i, e or "SS")
            elif kind == "Y":
                turn_y(h, i, e or "SS")
            elif kind == "y":
                quantize_y(h, i)
            elif kind == "O":
                stage3(h, i, e or "SSSS")
            elif kind == "g":
                turn_gains()
            elif kind == "N":
                skip_x(h, i)
            elif kind == "Z":
                stage1(h, i)

        for u in PRO.split():
            unit(u)
        steps = [(h, g) for h in range(len(CHUNKS)) for g in range(G)]
        for s in range(len(steps) + 1):
            this = steps[s] if s < len(steps) else None
            prev = steps[s - 1] if s > 0 else None
            nxt = steps[s + 1] if s + 1 < len(steps) else None
            if nxt:
                skip_x(*nxt)
            if this:
                finish1(*this)
            for u in PRE[s].split():
                unit(u)
            if this and CAST[s] == "V":
                cast_z("V", *this)
            if prev:
                quantize_z(*prev)
                stage2(*prev)
            if this and CAST[s] != "V":
                cast_z(CAST[s], *this)
            if this:
                skip_z(*this)
            for u in MID[s].split():
                unit(u)
            if nxt:
                stage1(*nxt)
            if prev:
                finish2(*prev, range(G))
            for u in POST[s].split():
                unit(u)
        for u in END.split():
            unit(u)
